import numpy as np
import ml_dtypes


def mxq(x, axis, fmt="e4m3"):
    dtype, down = {"e4m3": (ml_dtypes.float8_e4m3fn, 7), "e5m2": (ml_dtypes.float8_e5m2, 14)}[fmt]
    v = np.moveaxis(np.asarray(x, np.float32).astype(ml_dtypes.bfloat16).astype(np.float64), axis, -1)
    blocks = v.reshape(v.shape[:-1] + (-1, 32))
    amax = np.abs(blocks).max(-1, keepdims=True)
    byte = np.maximum(np.where(amax > 0, np.frexp(amax)[1] - 1 + 127, 0) - down, 1)
    scale = np.exp2(byte - 127.0)
    codes = (blocks / scale).astype(np.float32).astype(dtype).astype(np.float64)
    return np.moveaxis((codes * scale).reshape(v.shape), -1, axis)


WIDE = False


def mx_kscale(k):
    if not WIDE:
        return np.ones(k)
    levels = np.array([10, -10, 5, -5, 0])
    if k % 512:
        return np.exp2(np.random.permutation(np.resize(levels, k // 32))).repeat(32)
    a = np.empty((k // 512, 16))
    for p in range(k // 512):
        a[p, :8] = np.random.permutation(np.resize(levels, 8))
        for g in range(8):
            far = levels[np.abs(levels - a[p, g]) >= 10]
            a[p, g + 8] = far[np.random.randint(len(far))]
    return np.exp2(a.ravel()).repeat(32)


def f64(x):
    return np.asarray(x).astype(np.float64)


def striped(idx):
    return np.tile(idx.reshape(-1, 16).T, (8, 1)).astype(np.uint16)


def unstriped(offs):
    return offs[:16].T.reshape(-1).astype(np.int64)


def pack_weight(w):
    k, n = w.shape
    w = f64(np.asarray(w, np.float32).astype(ml_dtypes.bfloat16)).reshape(k // 32, 32, n)
    amax = np.abs(w).max(1)
    byte = np.clip(np.where(amax > 0, np.frexp(amax)[1] - 1 + 127 - 7, 1), 1, 254)
    scaled = (w * np.exp2(127.0 - byte)[:, None, :]).reshape(k, n).astype(np.float32)
    words = np.ascontiguousarray(scaled.reshape(k // 512, 128, 4, n).transpose(0, 1, 3, 2)).astype(ml_dtypes.float8_e4m3fn).view(np.uint8)
    return words, np.ascontiguousarray(byte.astype(np.uint8).reshape(k // 512, 16, n))


def unpack_weight(words, scales):
    g, p, n, _ = words.shape
    vals = np.ascontiguousarray(words).view(ml_dtypes.float8_e4m3fn).astype(np.float64) * np.repeat(np.exp2(scales.astype(np.float64) - 127.0), 8, axis=1)[..., None]
    return vals.transpose(0, 1, 3, 2).reshape(g * 512, n)


def relu(v):
    return np.maximum(v, 0.0)


K, T, S, H, N = 1024, 2048, 512, 512, 128
P = 2 ** 7


def setup_inputs():
    n = np.random.standard_normal
    s = mx_kscale(K)[:, None]
    u = mx_kscale(H)
    packed_xT = pack_weight(n((K, T)) * s)
    return {
        "x_words": packed_xT[0],
        "x_scales": packed_xT[1],
        "w1": (n((K, H)) / np.sqrt(K) / s * u).astype(np.float32),
        "w2": (n((H, N)) / np.sqrt(H) / u[:, None]).astype(np.float32),
        "in1": (np.tile((np.arange(S) % 4 >= 1) * 1.0, (P, 1))).astype(np.float32),
        "in2": (np.tile((np.arange(S) % 4 >= 2) * 1.0, (P, 1))).astype(np.float32),
        "offs": striped(np.random.permutation(T)[:S]),
    }


def reference(x_words, x_scales, w1, w2, in1, in2, offs):
    xq = unpack_weight(x_words, x_scales)[:, unstriped(offs)]
    h = relu(mxq(f64(w1), 0, "e4m3").T @ xq)
    y = mxq(f64(w2), 0, "e4m3").T @ mxq(h, 0, "e4m3")
    e0 = np.exp(y)
    e1 = e0 + (np.pad(e0, ((0, 0), (1, 0)))[:, :S]) * f64(in1)[:1]
    e2 = e1 + (np.pad(e1, ((0, 0), (2, 0)))[:, :S]) * f64(in2)[:1]
    return np.log(e2) - y

@@ -1,0 +1,158 @@
+from contextlib import ExitStack
+
+import concourse.mybir as mybir
+
+F32 = mybir.dt.float32
+BF16 = mybir.dt.bfloat16
+I32 = mybir.dt.int32
+U32 = mybir.dt.uint32
+U16 = mybir.dt.uint16
+U8 = mybir.dt.uint8
+FP8X4 = mybir.dt.float8_e4m3fn_x4
+ACT = mybir.ActivationFunctionType
+ALU = mybir.AluOpType
+
+K, T, S, H, N = 1024, 2048, 512, 512, 128
+P = 128
+PACK = 4
+K_PASS = P * PACK
+PASSES = K // K_PASS
+CHUNK = 128
+CHUNKS = S // CHUNK
+HALF = 256
+LIST_ROWS = 16
+PAD = 8
+BANK = 512
+VECTOR_CHUNK = 2
+FLOPS = 2 * K * H * S + 2 * H * N * S
+
+
+def tile_picked_ypl_terms_p_kernel(tc, x_words, x_scales, w1, w2, in1, in2, offs, out):
+    nc = tc.nc
+    with ExitStack() as ctx:
+        sb = ctx.enter_context(tc.tile_pool(name="sb", bufs=1))
+        psum = ctx.enter_context(tc.psum_pool(name="psum", bufs=1))
+
+        offsets = sb.tile([P, S // LIST_ROWS], U16, name="offsets")
+        nc.sync.dma_start(offsets[:], offs)
+
+        w1_raw = [sb.tile([P, PACK, H], F32, name=f"w1_raw{o}") for o in range(PASSES)]
+        scale_table = sb.tile([P, T], U8, name="scale_table", align_bytes=64)
+        nc.vector.memset(scale_table[:].bitcast(I32), 0)
+        for o in range(PASSES):
+            nc.sync.dma_start(w1_raw[o][:], w1[o * K_PASS : (o + 1) * K_PASS, :].rearrange("(p j) c -> p j c", j=PACK))
+            if o == 0:
+                for q in range(4):
+                    nc.sync.dma_start(scale_table[32 * q : 32 * q + 4 * PASSES, :].bitcast(I32), x_scales[:, 4 * q : 4 * q + 4, :].bitcast(I32))
+        x_table = [sb.tile([P, T], I32, name=f"x_table{o}", align_bytes=64) for o in range(PASSES)]
+        for o in range(PASSES):
+            nc.sync.dma_start(x_table[o][:], x_words[o].rearrange("p n t -> p (n t)").bitcast(I32))
+        w2_raw = sb.tile([P, PACK, N], F32, name="w2_raw")
+        nc.sync.dma_start(w2_raw[:], w2.rearrange("(p j) m -> p j m", j=PACK))
+        mask1 = sb.tile([P, S], F32, name="mask1")
+        nc.sync.dma_start(mask1[:], in1)
+        mask2 = sb.tile([P, S], F32, name="mask2")
+        nc.sync.dma_start(mask2[:], in2)
+
+        e0 = sb.tile([P, PAD + S], F32, name="e0")
+        e1 = sb.tile([P, PAD + S], F32, name="e1")
+        nc.vector.memset(e0[:, 0:PAD], 0.0)
+        nc.vector.memset(e1[:, 0:PAD], 0.0)
+
+        w1_codes, w1_planes = {}, {}
+        for o in range(PASSES):
+            src = w1_raw[o][:].rearrange("p j (m u t) -> p u m t j", u=2, t=2)
+            for u in range(2):
+                grouped = sb.tile([P, 2, P, PACK], BF16, name=f"w1_grouped{o}{u}", align_bytes=64)
+                dst = grouped[:].rearrange("p t m j -> p m t j")
+                if u == 0:
+                    nc.vector.tensor_copy(dst, src[:, u])
+                else:
+                    nc.scalar.copy(dst, src[:, u])
+                codes = sb.tile([P, 2 * P], U32, name=f"w1_codes{o}{u}", align_bytes=64)
+                plane = sb.tile([P, 2 * P], U8, name=f"w1_plane{o}{u}", align_bytes=64)
+                nc.vector.quantize_mx(out=codes[:].bitcast(FP8X4), scales=plane[:], in_=grouped[:].rearrange("p t m j -> p (t m j)"))
+                for t in range(2):
+                    w1_codes[(o, 2 * u + t)] = codes[:, t * P : (t + 1) * P]
+                    w1_planes[(o, 2 * u + t)] = plane[:, t * P : (t + 1) * P]
+
+        x_plane = sb.tile([P, S], U8, name="x_plane", align_bytes=64)
+        nc.vector.tensor_copy(x_plane[:], scale_table[:].indirect(offsets[:]))
+        x_codes = {}
+        for o in range(PASSES):
+            for half in range(S // HALF):
+                picked = sb.tile([P, HALF], U32, name=f"picked{o}{half}", align_bytes=64)
+                cols = slice(half * HALF // LIST_ROWS, (half + 1) * HALF // LIST_ROWS)
+                nc.vector.tensor_copy(picked[:], x_table[o][:].bitcast(U32).indirect(offsets[:, cols]))
+                for i in range(HALF // CHUNK):
+                    x_codes[(o, half * (HALF // CHUNK) + i)] = picked[:, i * CHUNK : (i + 1) * CHUNK]
+
+        w2_grouped = sb.tile([P, N, PACK], BF16, name="w2_grouped", align_bytes=64)
+        nc.scalar.copy(w2_grouped[:], w2_raw[:].rearrange("p j m -> p m j"))
+        w2_codes = sb.tile([P, N], U32, name="w2_codes", align_bytes=64)
+        w2_plane = sb.tile([P, N], U8, name="w2_plane", align_bytes=64)
+        nc.vector.quantize_mx(out=w2_codes[:].bitcast(FP8X4), scales=w2_plane[:], in_=w2_grouped[:].rearrange("p m j -> p (m j)"))
+
+        h_banks = [psum.tile([P, PACK, CHUNK], F32, name=f"h_bank{c}") for c in range(CHUNKS)]
+        y_banks = [psum.tile([P, BANK], F32, name=f"y_bank{c}") for c in range(CHUNKS)]
+
+        def first_product(c, t, o):
+            nc.tensor.matmul_mx(
+                out=h_banks[c][:, t, :],
+                lhsT=w1_codes[(o, t)].bitcast(FP8X4),
+                lhsT_scale=w1_planes[(o, t)],
+                rhs=x_codes[(o, c)].bitcast(FP8X4),
+                rhs_scale=x_plane[4 * o : P, c * CHUNK : (c + 1) * CHUNK],
+                start=(o == 0),
+                stop=(o == PASSES - 1),
+            )
+
+        for c in range(CHUNKS):
+            first_product(c, 0, 0)
+
+        for c in range(CHUNKS):
+            first_product(c, 0, 1)
+            for t in range(1, PACK):
+                for o in range(PASSES):
+                    first_product(c, t, o)
+            h_grouped = sb.tile([P, CHUNK, PACK], BF16, name=f"h_grouped{c}", align_bytes=64)
+            if c == VECTOR_CHUNK:
+                nc.vector.tensor_scalar_max(h_grouped[:], h_banks[c][:].rearrange("p t n -> p n t"), 0.0)
+            else:
+                nc.scalar.activation(h_grouped[:], h_banks[c][:].rearrange("p t n -> p n t"), ACT.Relu)
+            h_codes = sb.tile([P, CHUNK], U32, name=f"h_codes{c}", align_bytes=64)
+            h_plane = sb.tile([P, CHUNK], U8, name=f"h_plane{c}", align_bytes=64)
+            nc.vector.quantize_mx(out=h_codes[:].bitcast(FP8X4), scales=h_plane[:], in_=h_grouped[:].rearrange("p n t -> p (n t)"))
+            nc.tensor.matmul_mx(
+                out=y_banks[c][:, 0:CHUNK],
+                lhsT=w2_codes[:].bitcast(FP8X4),
+                lhsT_scale=w2_plane[:],
+                rhs=h_codes[:].bitcast(FP8X4),
+                rhs_scale=h_plane[:],
+                start=True,
+                stop=True,
+            )
+
+        for c in range(CHUNKS):
+            nc.scalar.activation(e0[:, PAD + c * CHUNK : PAD + (c + 1) * CHUNK], y_banks[c][:, 0:CHUNK], ACT.Exp)
+
+        e2 = sb.tile([P, S], F32, name="e2")
+        for c in range(CHUNKS):
+            cols = slice(c * CHUNK, (c + 1) * CHUNK)
+            lo, hi = PAD + c * CHUNK, PAD + (c + 1) * CHUNK
+            term1 = sb.tile([P, CHUNK], F32, name=f"term1_{c}")
+            nc.vector.tensor_tensor(term1[:], e0[:, lo - 1 : hi - 1], mask1[:, cols], ALU.mult)
+            nc.vector.tensor_tensor(e1[:, lo:hi], e0[:, lo:hi], term1[:], ALU.add)
+            term2 = sb.tile([P, CHUNK], F32, name=f"term2_{c}")
+            nc.vector.tensor_tensor(term2[:], e1[:, lo - 2 : hi - 2], mask2[:, cols], ALU.mult)
+            nc.vector.tensor_tensor(e2[:, cols], e1[:, lo:hi], term2[:], ALU.add)
+
+        result = sb.tile([P, S], F32, name="result")
+        for half in range(S // HALF):
+            cols = slice(half * HALF, (half + 1) * HALF)
+            other = PAD + (1 - half) * HALF
+            nc.scalar.activation(e0[:, other : other + HALF], e2[:, cols], ACT.Ln)
+            for i in range(HALF // CHUNK):
+                c = half * (HALF // CHUNK) + i
+                nc.vector.tensor_tensor(result[:, c * CHUNK : (c + 1) * CHUNK], e0[:, other + i * CHUNK : other + (i + 1) * CHUNK], y_banks[c][:, 0:CHUNK], ALU.subtract)
+            nc.sync.dma_start(out[:, cols], result[:, cols])

@@ -23,6 +23,8 @@ HALF = 256
 LIST_ROWS = 16
 PAD = 8
 BANK = 512
+LAG = 2
+WARM_UP_PASSES = 4
 VECTOR_CHUNK = 2
 FLOPS = 2 * K * H * S + 2 * H * N * S
 
@@ -33,17 +35,17 @@ def tile_picked_ypl_terms_p_kernel(tc, x_words, x_scales, w1, w2, in1, in2, offs
         sb = ctx.enter_context(tc.tile_pool(name="sb", bufs=1))
         psum = ctx.enter_context(tc.psum_pool(name="psum", bufs=1))
 
-        offsets = sb.tile([P, S // LIST_ROWS], U16, name="offsets")
-        nc.sync.dma_start(offsets[:], offs)
+        scale_table = sb.tile([P, T], U8, name="scale_table", align_bytes=64)
+        nc.gpsimd.memset(scale_table[:, 0 : T // 2].bitcast(I32), 0)
+        nc.vector.memset(scale_table[:, T // 2 : T].bitcast(I32), 0)
 
         w1_raw = [sb.tile([P, PACK, H], F32, name=f"w1_raw{o}") for o in range(PASSES)]
-        scale_table = sb.tile([P, T], U8, name="scale_table", align_bytes=64)
-        nc.vector.memset(scale_table[:].bitcast(I32), 0)
-        for o in range(PASSES):
-            nc.sync.dma_start(w1_raw[o][:], w1[o * K_PASS : (o + 1) * K_PASS, :].rearrange("(p j) c -> p j c", j=PACK))
-            if o == 0:
-                for q in range(4):
-                    nc.sync.dma_start(scale_table[32 * q : 32 * q + 4 * PASSES, :].bitcast(I32), x_scales[:, 4 * q : 4 * q + 4, :].bitcast(I32))
+        nc.sync.dma_start(w1_raw[0][:], w1[0:K_PASS, :].rearrange("(p j) c -> p j c", j=PACK))
+        offsets = sb.tile([P, S // LIST_ROWS], U16, name="offsets")
+        nc.sync.dma_start(offsets[:], offs)
+        for q in range(4):
+            nc.sync.dma_start(scale_table[32 * q : 32 * q + 4 * PASSES, :].bitcast(I32), x_scales[:, 4 * q : 4 * q + 4, :].bitcast(I32))
+        nc.sync.dma_start(w1_raw[1][:], w1[K_PASS:K, :].rearrange("(p j) c -> p j c", j=PACK))
         x_table = [sb.tile([P, T], I32, name=f"x_table{o}", align_bytes=64) for o in range(PASSES)]
         for o in range(PASSES):
             nc.sync.dma_start(x_table[o][:], x_words[o].rearrange("p n t -> p (n t)").bitcast(I32))
@@ -78,10 +80,11 @@ def tile_picked_ypl_terms_p_kernel(tc, x_words, x_scales, w1, w2, in1, in2, offs
 
         x_plane = sb.tile([P, S], U8, name="x_plane", align_bytes=64)
         nc.vector.tensor_copy(x_plane[:], scale_table[:].indirect(offsets[:]))
-        x_codes = {}
+        x_codes, picked_halves = {}, {}
         for o in range(PASSES):
             for half in range(S // HALF):
                 picked = sb.tile([P, HALF], U32, name=f"picked{o}{half}", align_bytes=64)
+                picked_halves[(o, half)] = picked
                 cols = slice(half * HALF // LIST_ROWS, (half + 1) * HALF // LIST_ROWS)
                 nc.vector.tensor_copy(picked[:], x_table[o][:].bitcast(U32).indirect(offsets[:, cols]))
                 for i in range(HALF // CHUNK):
@@ -107,8 +110,32 @@ def tile_picked_ypl_terms_p_kernel(tc, x_words, x_scales, w1, w2, in1, in2, offs
                 stop=(o == PASSES - 1),
             )
 
+        h_quantised = []
+
+        def second_product(c):
+            h_codes, h_plane = h_quantised[c]
+            nc.tensor.matmul_mx(
+                out=y_banks[c][:, 0:CHUNK],
+                lhsT=w2_codes[:].bitcast(FP8X4),
+                lhsT_scale=w2_plane[:],
+                rhs=h_codes[:].bitcast(FP8X4),
+                rhs_scale=h_plane[:],
+                start=True,
+                stop=True,
+            )
+
         for c in range(CHUNKS):
             first_product(c, 0, 0)
+        for t in range(WARM_UP_PASSES):
+            nc.tensor.matmul_mx(
+                out=y_banks[CHUNKS - 1][:, 0:HALF],
+                lhsT=w1_codes[(0, t)].bitcast(FP8X4),
+                lhsT_scale=w1_planes[(0, t)],
+                rhs=picked_halves[(0, 0)][:].bitcast(FP8X4),
+                rhs_scale=x_plane[:, 0:HALF],
+                start=True,
+                stop=True,
+            )
 
         for c in range(CHUNKS):
             first_product(c, 0, 1)
@@ -123,15 +150,11 @@ def tile_picked_ypl_terms_p_kernel(tc, x_words, x_scales, w1, w2, in1, in2, offs
             h_codes = sb.tile([P, CHUNK], U32, name=f"h_codes{c}", align_bytes=64)
             h_plane = sb.tile([P, CHUNK], U8, name=f"h_plane{c}", align_bytes=64)
             nc.vector.quantize_mx(out=h_codes[:].bitcast(FP8X4), scales=h_plane[:], in_=h_grouped[:].rearrange("p n t -> p (n t)"))
-            nc.tensor.matmul_mx(
-                out=y_banks[c][:, 0:CHUNK],
-                lhsT=w2_codes[:].bitcast(FP8X4),
-                lhsT_scale=w2_plane[:],
-                rhs=h_codes[:].bitcast(FP8X4),
-                rhs_scale=h_plane[:],
-                start=True,
-                stop=True,
-            )
+            h_quantised.append((h_codes, h_plane))
+            if c >= LAG:
+                second_product(c - LAG)
+        for c in range(CHUNKS - LAG, CHUNKS):
+            second_product(c)
 
         for c in range(CHUNKS):
             nc.scalar.activation(e0[:, PAD + c * CHUNK : PAD + (c + 1) * CHUNK], y_banks[c][:, 0:CHUNK], ACT.Exp)

@@ -17,14 +17,15 @@ P = 128
 PACK = 4
 K_PASS = P * PACK
 PASSES = K // K_PASS
+QUADRANT = 32
+PLANE_ROWS = 4
+LIST_ROWS = 16
 CHUNK = 128
 CHUNKS = S // CHUNK
 HALF = 256
-LIST_ROWS = 16
 PAD = 8
 BANK = 512
 LAG = 2
-WARM_UP_PASSES = 4
 VECTOR_CHUNK = 2
 FLOPS = 2 * K * H * S + 2 * H * N * S
 
@@ -43,12 +44,15 @@ def tile_picked_ypl_terms_p_kernel(tc, x_words, x_scales, w1, w2, in1, in2, offs
         nc.sync.dma_start(w1_raw[0][:], w1[0:K_PASS, :].rearrange("(p j) c -> p j c", j=PACK))
         offsets = sb.tile([P, S // LIST_ROWS], U16, name="offsets")
         nc.sync.dma_start(offsets[:], offs)
-        for q in range(4):
-            nc.sync.dma_start(scale_table[32 * q : 32 * q + 4 * PASSES, :].bitcast(I32), x_scales[:, 4 * q : 4 * q + 4, :].bitcast(I32))
+        for q in range(P // QUADRANT):
+            nc.sync.dma_start(
+                scale_table[QUADRANT * q : QUADRANT * q + PLANE_ROWS * PASSES, :].bitcast(I32),
+                x_scales[:, PLANE_ROWS * q : PLANE_ROWS * (q + 1), :].bitcast(I32),
+            )
         nc.sync.dma_start(w1_raw[1][:], w1[K_PASS:K, :].rearrange("(p j) c -> p j c", j=PACK))
         x_table = [sb.tile([P, T], I32, name=f"x_table{o}", align_bytes=64) for o in range(PASSES)]
         for o in range(PASSES):
-            nc.sync.dma_start(x_table[o][:], x_words[o].rearrange("p n t -> p (n t)").bitcast(I32))
+            nc.sync.dma_start(x_table[o][:], x_words[o].rearrange("p n j -> p (n j)").bitcast(I32))
         w2_raw = sb.tile([P, PACK, N], F32, name="w2_raw")
         nc.sync.dma_start(w2_raw[:], w2.rearrange("(p j) m -> p j m", j=PACK))
         mask1 = sb.tile([P, S], F32, name="mask1")
@@ -63,32 +67,26 @@ def tile_picked_ypl_terms_p_kernel(tc, x_words, x_scales, w1, w2, in1, in2, offs
 
         w1_codes, w1_planes = {}, {}
         for o in range(PASSES):
-            src = w1_raw[o][:].rearrange("p j (m u t) -> p u m t j", u=2, t=2)
+            dealt = w1_raw[o][:].rearrange("p j (m u v) -> p u m v j", u=2, v=2)
             for u in range(2):
                 grouped = sb.tile([P, 2, P, PACK], BF16, name=f"w1_grouped{o}{u}", align_bytes=64)
-                dst = grouped[:].rearrange("p t m j -> p m t j")
-                if u == 0:
-                    nc.vector.tensor_copy(dst, src[:, u])
-                else:
-                    nc.scalar.copy(dst, src[:, u])
+                interleave = nc.vector.tensor_copy if u == 0 else nc.scalar.copy
+                interleave(grouped[:].rearrange("p v m j -> p m v j"), dealt[:, u])
                 codes = sb.tile([P, 2 * P], U32, name=f"w1_codes{o}{u}", align_bytes=64)
                 plane = sb.tile([P, 2 * P], U8, name=f"w1_plane{o}{u}", align_bytes=64)
-                nc.vector.quantize_mx(out=codes[:].bitcast(FP8X4), scales=plane[:], in_=grouped[:].rearrange("p t m j -> p (t m j)"))
-                for t in range(2):
-                    w1_codes[(o, 2 * u + t)] = codes[:, t * P : (t + 1) * P]
-                    w1_planes[(o, 2 * u + t)] = plane[:, t * P : (t + 1) * P]
+                nc.vector.quantize_mx(out=codes[:].bitcast(FP8X4), scales=plane[:], in_=grouped[:].rearrange("p v m j -> p (v m j)"))
+                for v in range(2):
+                    w1_codes[(o, 2 * u + v)] = codes[:, v * P : (v + 1) * P]
+                    w1_planes[(o, 2 * u + v)] = plane[:, v * P : (v + 1) * P]
 
         x_plane = sb.tile([P, S], U8, name="x_plane", align_bytes=64)
         nc.vector.tensor_copy(x_plane[:], scale_table[:].indirect(offsets[:]))
-        x_codes, picked_halves = {}, {}
+        picked = {}
         for o in range(PASSES):
             for half in range(S // HALF):
-                picked = sb.tile([P, HALF], U32, name=f"picked{o}{half}", align_bytes=64)
-                picked_halves[(o, half)] = picked
-                cols = slice(half * HALF // LIST_ROWS, (half + 1) * HALF // LIST_ROWS)
-                nc.vector.tensor_copy(picked[:], x_table[o][:].bitcast(U32).indirect(offsets[:, cols]))
-                for i in range(HALF // CHUNK):
-                    x_codes[(o, half * (HALF // CHUNK) + i)] = picked[:, i * CHUNK : (i + 1) * CHUNK]
+                picked[(o, half)] = sb.tile([P, HALF], U32, name=f"picked{o}{half}", align_bytes=64)
+                entries = offsets[:, half * HALF // LIST_ROWS : (half + 1) * HALF // LIST_ROWS]
+                nc.vector.tensor_copy(picked[(o, half)][:], x_table[o][:].bitcast(U32).indirect(entries))
 
         w2_grouped = sb.tile([P, N, PACK], BF16, name="w2_grouped", align_bytes=64)
         nc.scalar.copy(w2_grouped[:], w2_raw[:].rearrange("p j m -> p m j"))
@@ -98,19 +96,19 @@ def tile_picked_ypl_terms_p_kernel(tc, x_words, x_scales, w1, w2, in1, in2, offs
 
         h_banks = [psum.tile([P, PACK, CHUNK], F32, name=f"h_bank{c}") for c in range(CHUNKS)]
         y_banks = [psum.tile([P, BANK], F32, name=f"y_bank{c}") for c in range(CHUNKS)]
+        h_quantised = []
 
         def first_product(c, t, o):
+            half, first = divmod(c * CHUNK, HALF)
             nc.tensor.matmul_mx(
                 out=h_banks[c][:, t, :],
                 lhsT=w1_codes[(o, t)].bitcast(FP8X4),
                 lhsT_scale=w1_planes[(o, t)],
-                rhs=x_codes[(o, c)].bitcast(FP8X4),
-                rhs_scale=x_plane[4 * o : P, c * CHUNK : (c + 1) * CHUNK],
+                rhs=picked[(o, half)][:, first : first + CHUNK].bitcast(FP8X4),
+                rhs_scale=x_plane[PLANE_ROWS * o : P, c * CHUNK : (c + 1) * CHUNK],
                 start=(o == 0),
                 stop=(o == PASSES - 1),
             )
-
-        h_quantised = []
 
         def second_product(c):
             h_codes, h_plane = h_quantised[c]
@@ -126,16 +124,6 @@ def tile_picked_ypl_terms_p_kernel(tc, x_words, x_scales, w1, w2, in1, in2, offs
 
         for c in range(CHUNKS):
             first_product(c, 0, 0)
-        for t in range(WARM_UP_PASSES):
-            nc.tensor.matmul_mx(
-                out=y_banks[CHUNKS - 1][:, 0:HALF],
-                lhsT=w1_codes[(0, t)].bitcast(FP8X4),
-                lhsT_scale=w1_planes[(0, t)],
-                rhs=picked_halves[(0, 0)][:].bitcast(FP8X4),
-                rhs_scale=x_plane[:, 0:HALF],
-                start=True,
-                stop=True,
-            )
 
         for c in range(CHUNKS):
             first_product(c, 0, 1)
@@ -172,10 +160,11 @@ def tile_picked_ypl_terms_p_kernel(tc, x_words, x_scales, w1, w2, in1, in2, offs
 
         result = sb.tile([P, S], F32, name="result")
         for half in range(S // HALF):
-            cols = slice(half * HALF, (half + 1) * HALF)
-            other = PAD + (1 - half) * HALF
-            nc.scalar.activation(e0[:, other : other + HALF], e2[:, cols], ACT.Ln)
+            half_cols = slice(half * HALF, (half + 1) * HALF)
+            log_start = PAD + (1 - half) * HALF
+            nc.scalar.activation(e0[:, log_start : log_start + HALF], e2[:, half_cols], ACT.Ln)
             for i in range(HALF // CHUNK):
                 c = half * (HALF // CHUNK) + i
-                nc.vector.tensor_tensor(result[:, c * CHUNK : (c + 1) * CHUNK], e0[:, other + i * CHUNK : other + (i + 1) * CHUNK], y_banks[c][:, 0:CHUNK], ALU.subtract)
-            nc.sync.dma_start(out[:, cols], result[:, cols])
+                log_sum = e0[:, log_start + i * CHUNK : log_start + (i + 1) * CHUNK]
+                nc.vector.tensor_tensor(result[:, c * CHUNK : (c + 1) * CHUNK], log_sum, y_banks[c][:, 0:CHUNK], ALU.subtract)
+            nc.sync.dma_start(out[:, half_cols], result[:, half_cols])

@@ -26,7 +26,6 @@ HALF = 256
 PAD = 8
 BANK = 512
 LAG = 2
-VECTOR_CHUNK = 2
 FLOPS = 2 * K * H * S + 2 * H * N * S
 
 
@@ -106,8 +105,8 @@ def tile_picked_ypl_terms_p_kernel(tc, x_words, x_scales, w1, w2, in1, in2, offs
                 lhsT_scale=w1_planes[(o, t)],
                 rhs=picked[(o, half)][:, first : first + CHUNK].bitcast(FP8X4),
                 rhs_scale=x_plane[PLANE_ROWS * o : P, c * CHUNK : (c + 1) * CHUNK],
-                start=(o == 0),
-                stop=(o == PASSES - 1),
+                start=(o == 0 and t == 0),
+                stop=(o == PASSES - 1 and t == PACK - 1),
             )
 
         def second_product(c):
@@ -123,15 +122,14 @@ def tile_picked_ypl_terms_p_kernel(tc, x_words, x_scales, w1, w2, in1, in2, offs
             )
 
         for c in range(CHUNKS):
-            first_product(c, 0, 0)
+            for t in range(PACK):
+                first_product(c, t, 0)
 
         for c in range(CHUNKS):
-            first_product(c, 0, 1)
-            for t in range(1, PACK):
-                for o in range(PASSES):
-                    first_product(c, t, o)
+            for t in range(PACK):
+                first_product(c, t, 1)
             h_grouped = sb.tile([P, CHUNK, PACK], BF16, name=f"h_grouped{c}", align_bytes=64)
-            if c == VECTOR_CHUNK:
+            if c % 2 == 1:
                 nc.vector.tensor_scalar_max(h_grouped[:], h_banks[c][:].rearrange("p t n -> p n t"), 0.0)
             else:
                 nc.scalar.activation(h_grouped[:], h_banks[c][:].rearrange("p t n -> p n t"), ACT.Relu)
@@ -148,15 +146,18 @@ def tile_picked_ypl_terms_p_kernel(tc, x_words, x_scales, w1, w2, in1, in2, offs
             nc.scalar.activation(e0[:, PAD + c * CHUNK : PAD + (c + 1) * CHUNK], y_banks[c][:, 0:CHUNK], ACT.Exp)
 
         e2 = sb.tile([P, S], F32, name="e2")
-        for c in range(CHUNKS):
-            cols = slice(c * CHUNK, (c + 1) * CHUNK)
-            lo, hi = PAD + c * CHUNK, PAD + (c + 1) * CHUNK
-            term1 = sb.tile([P, CHUNK], F32, name=f"term1_{c}")
-            nc.vector.tensor_tensor(term1[:], e0[:, lo - 1 : hi - 1], mask1[:, cols], ALU.mult)
-            nc.vector.tensor_tensor(e1[:, lo:hi], e0[:, lo:hi], term1[:], ALU.add)
-            term2 = sb.tile([P, CHUNK], F32, name=f"term2_{c}")
-            nc.vector.tensor_tensor(term2[:], e1[:, lo - 2 : hi - 2], mask2[:, cols], ALU.mult)
-            nc.vector.tensor_tensor(e2[:, cols], e1[:, lo:hi], term2[:], ALU.add)
+        term1 = sb.tile([P, S], F32, name="term1")
+        term2 = sb.tile([P, S], F32, name="term2")
+        for pair in range(CHUNKS // 2):
+            spans = [(slice(c * CHUNK, (c + 1) * CHUNK), PAD + c * CHUNK, PAD + (c + 1) * CHUNK) for c in (2 * pair, 2 * pair + 1)]
+            for cols, lo, hi in spans:
+                nc.vector.tensor_tensor(term1[:, cols], e0[:, lo - 1 : hi - 1], mask1[:, cols], ALU.mult)
+            for cols, lo, hi in spans:
+                nc.vector.tensor_tensor(e1[:, lo:hi], e0[:, lo:hi], term1[:, cols], ALU.add)
+            for cols, lo, hi in spans:
+                nc.vector.tensor_tensor(term2[:, cols], e1[:, lo - 2 : hi - 2], mask2[:, cols], ALU.mult)
+            for cols, lo, hi in spans:
+                nc.vector.tensor_tensor(e2[:, cols], e1[:, lo:hi], term2[:, cols], ALU.add)
 
         result = sb.tile([P, S], F32, name="result")
         for half in range(S // HALF):

@@ -88,7 +88,7 @@ def tile_picked_ypl_terms_p_kernel(tc, x_words, x_scales, w1, w2, in1, in2, offs
                 nc.vector.tensor_copy(picked[(o, half)][:], x_table[o][:].bitcast(U32).indirect(entries))
 
         w2_grouped = sb.tile([P, N, PACK], BF16, name="w2_grouped", align_bytes=64)
-        nc.scalar.copy(w2_grouped[:], w2_raw[:].rearrange("p j m -> p m j"))
+        nc.gpsimd.tensor_scalar(w2_grouped[:], w2_raw[:].rearrange("p j m -> p m j"), 1.0, 0.0, ALU.mult, ALU.add)
         w2_codes = sb.tile([P, N], U32, name="w2_codes", align_bytes=64)
         w2_plane = sb.tile([P, N], U8, name="w2_plane", align_bytes=64)
         nc.vector.quantize_mx(out=w2_codes[:].bitcast(FP8X4), scales=w2_plane[:], in_=w2_grouped[:].rearrange("p m j -> p (m j)"))
@@ -129,7 +129,7 @@ def tile_picked_ypl_terms_p_kernel(tc, x_words, x_scales, w1, w2, in1, in2, offs
             for t in range(PACK):
                 first_product(c, t, 1)
             h_grouped = sb.tile([P, CHUNK, PACK], BF16, name=f"h_grouped{c}", align_bytes=64)
-            if c % 2 == 1:
+            if c == 2:
                 nc.vector.tensor_scalar_max(h_grouped[:], h_banks[c][:].rearrange("p t n -> p n t"), 0.0)
             else:
                 nc.scalar.activation(h_grouped[:], h_banks[c][:].rearrange("p t n -> p n t"), ACT.Relu)
@@ -160,12 +160,11 @@ def tile_picked_ypl_terms_p_kernel(tc, x_words, x_scales, w1, w2, in1, in2, offs
                 nc.vector.tensor_tensor(e2[:, cols], e1[:, lo:hi], term2[:, cols], ALU.add)
 
         result = sb.tile([P, S], F32, name="result")
-        for half in range(S // HALF):
-            half_cols = slice(half * HALF, (half + 1) * HALF)
-            log_start = PAD + (1 - half) * HALF
-            nc.scalar.activation(e0[:, log_start : log_start + HALF], e2[:, half_cols], ACT.Ln)
-            for i in range(HALF // CHUNK):
-                c = half * (HALF // CHUNK) + i
-                log_sum = e0[:, log_start + i * CHUNK : log_start + (i + 1) * CHUNK]
+        for first, last in ((0, 2), (2, 3), (3, 4)):
+            cols = slice(first * CHUNK, last * CHUNK)
+            log_start = PAD + (first * CHUNK + HALF) % S
+            nc.scalar.activation(e0[:, log_start : log_start + (last - first) * CHUNK], e2[:, cols], ACT.Ln)
+            for c in range(first, last):
+                log_sum = e0[:, log_start + (c - first) * CHUNK : log_start + (c - first + 1) * CHUNK]
                 nc.vector.tensor_tensor(result[:, c * CHUNK : (c + 1) * CHUNK], log_sum, y_banks[c][:, 0:CHUNK], ALU.subtract)
-            nc.sync.dma_start(out[:, half_cols], result[:, half_cols])
+            nc.sync.dma_start(out[:, cols], result[:, cols])

@@ -148,23 +148,31 @@ def tile_picked_ypl_terms_p_kernel(tc, x_words, x_scales, w1, w2, in1, in2, offs
         e2 = sb.tile([P, S], F32, name="e2")
         term1 = sb.tile([P, S], F32, name="term1")
         term2 = sb.tile([P, S], F32, name="term2")
-        for pair in range(CHUNKS // 2):
-            spans = [(slice(c * CHUNK, (c + 1) * CHUNK), PAD + c * CHUNK, PAD + (c + 1) * CHUNK) for c in (2 * pair, 2 * pair + 1)]
-            for cols, lo, hi in spans:
+
+        def sum_stage(c, stage):
+            cols, lo, hi = slice(c * CHUNK, (c + 1) * CHUNK), PAD + c * CHUNK, PAD + (c + 1) * CHUNK
+            if stage == 0:
                 nc.vector.tensor_tensor(term1[:, cols], e0[:, lo - 1 : hi - 1], mask1[:, cols], ALU.mult)
-            for cols, lo, hi in spans:
+            elif stage == 1:
                 nc.vector.tensor_tensor(e1[:, lo:hi], e0[:, lo:hi], term1[:, cols], ALU.add)
-            for cols, lo, hi in spans:
+            elif stage == 2:
                 nc.vector.tensor_tensor(term2[:, cols], e1[:, lo - 2 : hi - 2], mask2[:, cols], ALU.mult)
-            for cols, lo, hi in spans:
+            else:
                 nc.vector.tensor_tensor(e2[:, cols], e1[:, lo:hi], term2[:, cols], ALU.add)
 
+        ahead = [(c, stage) for stage in range(4) for c in range(CHUNKS - 1)]
+        for i, (c, stage) in enumerate(ahead):
+            if i >= 6 and i % 2 == 0:
+                sum_stage(CHUNKS - 1, (i - 6) // 2)
+            sum_stage(c, stage)
+        sum_stage(CHUNKS - 1, 3)
+
         result = sb.tile([P, S], F32, name="result")
+        log_sum = sb.tile([P, S], F32, name="log_sum")
         for first, last in ((0, 2), (2, 3), (3, 4)):
-            cols = slice(first * CHUNK, last * CHUNK)
-            log_start = PAD + (first * CHUNK + HALF) % S
-            nc.scalar.activation(e0[:, log_start : log_start + (last - first) * CHUNK], e2[:, cols], ACT.Ln)
             for c in range(first, last):
-                log_sum = e0[:, log_start + (c - first) * CHUNK : log_start + (c - first + 1) * CHUNK]
-                nc.vector.tensor_tensor(result[:, c * CHUNK : (c + 1) * CHUNK], log_sum, y_banks[c][:, 0:CHUNK], ALU.subtract)
+                cols = slice(c * CHUNK, (c + 1) * CHUNK)
+                nc.scalar.activation(log_sum[:, cols], e2[:, cols], ACT.Ln)
+                nc.vector.tensor_tensor(result[:, cols], log_sum[:, cols], y_banks[c][:, 0:CHUNK], ALU.subtract)
+            cols = slice(first * CHUNK, last * CHUNK)
             nc.sync.dma_start(out[:, cols], result[:, cols])

@@ -19,6 +19,7 @@ K_PASS = P * PACK
 PASSES = K // K_PASS
 QUADRANT = 32
 PLANE_ROWS = 4
+SCALE_ROWS = 32
 LIST_ROWS = 16
 CHUNK = 128
 CHUNKS = S // CHUNK
@@ -35,34 +36,41 @@ def tile_picked_ypl_terms_p_kernel(tc, x_words, x_scales, w1, w2, in1, in2, offs
         sb = ctx.enter_context(tc.tile_pool(name="sb", bufs=1))
         psum = ctx.enter_context(tc.psum_pool(name="psum", bufs=1))
 
-        scale_table = sb.tile([P, T], U8, name="scale_table", align_bytes=64)
-        nc.gpsimd.memset(scale_table[:, 0 : T // 2].bitcast(I32), 0)
-        nc.vector.memset(scale_table[:, T // 2 : T].bitcast(I32), 0)
-
-        w1_raw = [sb.tile([P, PACK, H], F32, name=f"w1_raw{o}") for o in range(PASSES)]
-        nc.sync.dma_start(w1_raw[0][:], w1[0:K_PASS, :].rearrange("(p j) c -> p j c", j=PACK))
+        scale_table = sb.tile([P, T], U8, name="scale_table", tag="table_then_mask", align_bytes=64)
+        nc.sync.dma_start(scale_table[0:SCALE_ROWS, :].bitcast(I32), x_scales.rearrange("o g c -> g o c").bitcast(I32))
+        nc.gpsimd.memset(scale_table[QUADRANT : 2 * QUADRANT, :].bitcast(I32), 0)
+        nc.vector.memset(scale_table[2 * QUADRANT : P, :].bitcast(I32), 0)
+        x_plane = sb.tile([P, PASSES, S], U8, name="x_plane", align_bytes=64)
+        nc.gpsimd.memset(x_plane[:].rearrange("p o n -> p (o n)").bitcast(I32), 0)
         offsets = sb.tile([P, S // LIST_ROWS], U16, name="offsets")
         nc.sync.dma_start(offsets[:], offs)
-        for q in range(P // QUADRANT):
-            nc.sync.dma_start(
-                scale_table[QUADRANT * q : QUADRANT * q + PLANE_ROWS * PASSES, :].bitcast(I32),
-                x_scales[:, PLANE_ROWS * q : PLANE_ROWS * (q + 1), :].bitcast(I32),
-            )
-        nc.sync.dma_start(w1_raw[1][:], w1[K_PASS:K, :].rearrange("(p j) c -> p j c", j=PACK))
+        w1_raw = [sb.tile([P, PACK, H], F32, name=f"w1_raw{o}") for o in range(PASSES)]
+        for o in range(PASSES):
+            nc.sync.dma_start(w1_raw[o][:], w1[o * K_PASS : (o + 1) * K_PASS, :].rearrange("(p j) c -> p j c", j=PACK))
         x_table = [sb.tile([P, T], I32, name=f"x_table{o}", align_bytes=64) for o in range(PASSES)]
         for o in range(PASSES):
             nc.sync.dma_start(x_table[o][:], x_words[o].rearrange("p n j -> p (n j)").bitcast(I32))
         w2_raw = sb.tile([P, PACK, N], F32, name="w2_raw")
         nc.sync.dma_start(w2_raw[:], w2.rearrange("(p j) m -> p j m", j=PACK))
-        mask1 = sb.tile([P, S], F32, name="mask1")
+
+        picked_scales = sb.tile([P, S], U8, name="picked_scales", align_bytes=64)
+        nc.vector.tensor_copy(picked_scales[:], scale_table[:].indirect(offsets[:]))
+        rows = PASSES * PLANE_ROWS
+        for q in range(P // QUADRANT):
+            nc.scalar.dma_start(
+                x_plane[QUADRANT * q : QUADRANT * q + PLANE_ROWS].rearrange("p o n -> p (o n)").bitcast(I32),
+                picked_scales[rows * q : rows * (q + 1), :].bitcast(I32),
+            )
+
+        mask1 = sb.tile([P, S], F32, name="mask1", tag="table_then_mask", align_bytes=64)
         nc.sync.dma_start(mask1[:], in1)
         mask2 = sb.tile([P, S], F32, name="mask2")
         nc.sync.dma_start(mask2[:], in2)
 
         e0 = sb.tile([P, PAD + S], F32, name="e0")
         e1 = sb.tile([P, PAD + S], F32, name="e1")
-        nc.vector.memset(e0[:, 0:PAD], 0.0)
         nc.vector.memset(e1[:, 0:PAD], 0.0)
+        nc.scalar.copy(e0[:, 0:PAD], e1[:, 0:PAD])
 
         w1_codes, w1_planes = {}, {}
         for o in range(PASSES):
@@ -78,8 +86,6 @@ def tile_picked_ypl_terms_p_kernel(tc, x_words, x_scales, w1, w2, in1, in2, offs
                     w1_codes[(o, 2 * u + v)] = codes[:, v * P : (v + 1) * P]
                     w1_planes[(o, 2 * u + v)] = plane[:, v * P : (v + 1) * P]
 
-        x_plane = sb.tile([P, S], U8, name="x_plane", align_bytes=64)
-        nc.vector.tensor_copy(x_plane[:], scale_table[:].indirect(offsets[:]))
         picked = {}
         for o in range(PASSES):
             for half in range(S // HALF):
@@ -104,7 +110,7 @@ def tile_picked_ypl_terms_p_kernel(tc, x_words, x_scales, w1, w2, in1, in2, offs
                 lhsT=w1_codes[(o, t)].bitcast(FP8X4),
                 lhsT_scale=w1_planes[(o, t)],
                 rhs=picked[(o, half)][:, first : first + CHUNK].bitcast(FP8X4),
-                rhs_scale=x_plane[PLANE_ROWS * o : P, c * CHUNK : (c + 1) * CHUNK],
+                rhs_scale=x_plane[:, o, c * CHUNK : (c + 1) * CHUNK],
                 start=(o == 0 and t == 0),
                 stop=(o == PASSES - 1 and t == PACK - 1),
             )

@@ -1,6 +1,7 @@
 from contextlib import ExitStack
 
 import concourse.mybir as mybir
+from concourse.masks import make_identity
 
 F32 = mybir.dt.float32
 BF16 = mybir.dt.bfloat16
@@ -26,7 +27,9 @@ CHUNKS = S // CHUNK
 HALF = 256
 PAD = 8
 BANK = 512
-LAG = 2
+VECTOR_CHUNK = 1
+GPSIMD_ADDS = ()
+RATIO = ()
 FLOPS = 2 * K * H * S + 2 * H * N * S
 
 
@@ -36,7 +39,7 @@ def tile_picked_ypl_terms_p_kernel(tc, x_words, x_scales, w1, w2, in1, in2, offs
         sb = ctx.enter_context(tc.tile_pool(name="sb", bufs=1))
         psum = ctx.enter_context(tc.psum_pool(name="psum", bufs=1))
 
-        scale_table = sb.tile([P, T], U8, name="scale_table", tag="table_then_mask", align_bytes=64)
+        scale_table = sb.tile([P, T], U8, name="scale_table", align_bytes=64)
         nc.sync.dma_start(scale_table[0:SCALE_ROWS, :].bitcast(I32), x_scales.rearrange("o g c -> g o c").bitcast(I32))
         nc.gpsimd.memset(scale_table[QUADRANT : 2 * QUADRANT, :].bitcast(I32), 0)
         nc.vector.memset(scale_table[2 * QUADRANT : P, :].bitcast(I32), 0)
@@ -44,14 +47,33 @@ def tile_picked_ypl_terms_p_kernel(tc, x_words, x_scales, w1, w2, in1, in2, offs
         nc.gpsimd.memset(x_plane[:].rearrange("p o n -> p (o n)").bitcast(I32), 0)
         offsets = sb.tile([P, S // LIST_ROWS], U16, name="offsets")
         nc.sync.dma_start(offsets[:], offs)
-        w1_raw = [sb.tile([P, PACK, H], F32, name=f"w1_raw{o}") for o in range(PASSES)]
+        w1_raw = [sb.tile([P, PACK, H], F32, name=f"w1_raw{o}", tag=f"stage{o}", align_bytes=64) for o in range(PASSES)]
         for o in range(PASSES):
             nc.sync.dma_start(w1_raw[o][:], w1[o * K_PASS : (o + 1) * K_PASS, :].rearrange("(p j) c -> p j c", j=PACK))
-        x_table = [sb.tile([P, T], I32, name=f"x_table{o}", align_bytes=64) for o in range(PASSES)]
-        for o in range(PASSES):
-            nc.sync.dma_start(x_table[o][:], x_words[o].rearrange("p n j -> p (n j)").bitcast(I32))
-        w2_raw = sb.tile([P, PACK, N], F32, name="w2_raw")
-        nc.sync.dma_start(w2_raw[:], w2.rearrange("(p j) m -> p j m", j=PACK))
+        x_table = [sb.tile([P, T], I32, name="x_table0", align_bytes=64)]
+        nc.sync.dma_start(x_table[0][:], x_words[0].rearrange("p n j -> p (n j)").bitcast(I32))
+
+        e0 = sb.tile([P, PAD + S], F32, name="e0")
+        e1 = sb.tile([P, PAD + S], F32, name="e1")
+        nc.vector.memset(e1[:, 0:PAD], 0.0)
+        nc.scalar.copy(e0[:, 0:PAD], e1[:, 0:PAD])
+
+        mask_rows = sb.tile([P, CHUNK], F32, name="mask_rows")
+        nc.gpsimd.memset(mask_rows[:], 0.0)
+        identity = sb.tile([P, P], F32, name="identity")
+        make_identity(nc, identity[:])
+        for i, mask in enumerate((in1, in2)):
+            nc.scalar.dma_start(mask_rows[i * CHUNKS : (i + 1) * CHUNKS, :], mask[0].rearrange("(c n) -> c n", c=CHUNKS))
+        turned = psum.tile([P, BANK], F32, name="turned", tag="bank0")
+        nc.tensor.transpose(turned[:, 0:P], mask_rows[:], identity[:])
+        mask_cols = sb.tile([P, 2 * CHUNKS], F32, name="mask_cols")
+        nc.scalar.copy(mask_cols[:], turned[:, 0 : 2 * CHUNKS])
+        mask1 = psum.tile([P, S], F32, name="mask1")
+        mask2 = psum.tile([P, S], F32, name="mask2")
+        for i, mask in enumerate((mask1, mask2)):
+            for c in range(CHUNKS):
+                col = i * CHUNKS + c
+                nc.tensor.transpose(mask[:, c * CHUNK : (c + 1) * CHUNK], mask_cols[:, col : col + 1].to_broadcast([P, P]), identity[:])
 
         picked_scales = sb.tile([P, S], U8, name="picked_scales", align_bytes=64)
         nc.vector.tensor_copy(picked_scales[:], scale_table[:].indirect(offsets[:]))
@@ -61,16 +83,6 @@ def tile_picked_ypl_terms_p_kernel(tc, x_words, x_scales, w1, w2, in1, in2, offs
                 x_plane[QUADRANT * q : QUADRANT * q + PLANE_ROWS].rearrange("p o n -> p (o n)").bitcast(I32),
                 picked_scales[rows * q : rows * (q + 1), :].bitcast(I32),
             )
-
-        mask1 = sb.tile([P, S], F32, name="mask1", tag="table_then_mask", align_bytes=64)
-        nc.sync.dma_start(mask1[:], in1)
-        mask2 = sb.tile([P, S], F32, name="mask2")
-        nc.sync.dma_start(mask2[:], in2)
-
-        e0 = sb.tile([P, PAD + S], F32, name="e0")
-        e1 = sb.tile([P, PAD + S], F32, name="e1")
-        nc.vector.memset(e1[:, 0:PAD], 0.0)
-        nc.scalar.copy(e0[:, 0:PAD], e1[:, 0:PAD])
 
         w1_codes, w1_planes = {}, {}
         for o in range(PASSES):
@@ -86,6 +98,11 @@ def tile_picked_ypl_terms_p_kernel(tc, x_words, x_scales, w1, w2, in1, in2, offs
                     w1_codes[(o, 2 * u + v)] = codes[:, v * P : (v + 1) * P]
                     w1_planes[(o, 2 * u + v)] = plane[:, v * P : (v + 1) * P]
 
+        x_table.append(sb.tile([P, T], I32, name="x_table1", tag="stage0", align_bytes=64))
+        nc.sync.dma_start(x_table[1][:], x_words[1].rearrange("p n j -> p (n j)").bitcast(I32))
+        w2_raw = sb.tile([P, PACK, N], F32, name="w2_raw", tag="stage1", align_bytes=64)
+        nc.sync.dma_start(w2_raw[:], w2.rearrange("(p j) m -> p j m", j=PACK))
+
         picked = {}
         for o in range(PASSES):
             for half in range(S // HALF):
@@ -93,14 +110,13 @@ def tile_picked_ypl_terms_p_kernel(tc, x_words, x_scales, w1, w2, in1, in2, offs
                 entries = offsets[:, half * HALF // LIST_ROWS : (half + 1) * HALF // LIST_ROWS]
                 nc.vector.tensor_copy(picked[(o, half)][:], x_table[o][:].bitcast(U32).indirect(entries))
 
-        w2_grouped = sb.tile([P, N, PACK], BF16, name="w2_grouped", align_bytes=64)
+        w2_grouped = sb.tile([P, N, PACK], BF16, name="w2_grouped", tag="stage0", align_bytes=64)
         nc.gpsimd.tensor_scalar(w2_grouped[:], w2_raw[:].rearrange("p j m -> p m j"), 1.0, 0.0, ALU.mult, ALU.add)
         w2_codes = sb.tile([P, N], U32, name="w2_codes", align_bytes=64)
         w2_plane = sb.tile([P, N], U8, name="w2_plane", align_bytes=64)
-        nc.vector.quantize_mx(out=w2_codes[:].bitcast(FP8X4), scales=w2_plane[:], in_=w2_grouped[:].rearrange("p m j -> p (m j)"))
 
-        h_banks = [psum.tile([P, PACK, CHUNK], F32, name=f"h_bank{c}") for c in range(CHUNKS)]
-        y_banks = [psum.tile([P, BANK], F32, name=f"y_bank{c}") for c in range(CHUNKS)]
+        h_banks = [psum.tile([P, PACK, CHUNK], F32, name=f"h_bank{c}", tag=f"bank{c}") for c in range(CHUNKS)]
+        y_banks = {}
         h_quantised = []
 
         def first_product(c, t, o):
@@ -117,6 +133,7 @@ def tile_picked_ypl_terms_p_kernel(tc, x_words, x_scales, w1, w2, in1, in2, offs
 
         def second_product(c):
             h_codes, h_plane = h_quantised[c]
+            y_banks[c] = psum.tile([P, BANK], F32, name=f"y_bank{c}", tag=f"bank{c}")
             nc.tensor.matmul_mx(
                 out=y_banks[c][:, 0:CHUNK],
                 lhsT=w2_codes[:].bitcast(FP8X4),
@@ -127,58 +144,68 @@ def tile_picked_ypl_terms_p_kernel(tc, x_words, x_scales, w1, w2, in1, in2, offs
                 stop=True,
             )
 
-        for c in range(CHUNKS):
-            for t in range(PACK):
-                first_product(c, t, 0)
+        for o in range(PASSES):
+            for c in range(CHUNKS):
+                for t in range(PACK):
+                    first_product(c, t, o)
 
+        h_grouped = []
         for c in range(CHUNKS):
-            for t in range(PACK):
-                first_product(c, t, 1)
-            h_grouped = sb.tile([P, CHUNK, PACK], BF16, name=f"h_grouped{c}", align_bytes=64)
-            if c == 2:
-                nc.vector.tensor_scalar_max(h_grouped[:], h_banks[c][:].rearrange("p t n -> p n t"), 0.0)
+            h_grouped.append(sb.tile([P, CHUNK, PACK], BF16, name=f"h_grouped{c}", align_bytes=64))
+            if c == VECTOR_CHUNK:
+                nc.vector.tensor_scalar_max(h_grouped[c][:], h_banks[c][:].rearrange("p t n -> p n t"), 0.0)
             else:
-                nc.scalar.activation(h_grouped[:], h_banks[c][:].rearrange("p t n -> p n t"), ACT.Relu)
+                nc.scalar.activation(h_grouped[c][:], h_banks[c][:].rearrange("p t n -> p n t"), ACT.Relu)
+        for c in range(CHUNKS):
             h_codes = sb.tile([P, CHUNK], U32, name=f"h_codes{c}", align_bytes=64)
             h_plane = sb.tile([P, CHUNK], U8, name=f"h_plane{c}", align_bytes=64)
-            nc.vector.quantize_mx(out=h_codes[:].bitcast(FP8X4), scales=h_plane[:], in_=h_grouped[:].rearrange("p n t -> p (n t)"))
+            nc.vector.quantize_mx(out=h_codes[:].bitcast(FP8X4), scales=h_plane[:], in_=h_grouped[c][:].rearrange("p n t -> p (n t)"))
             h_quantised.append((h_codes, h_plane))
-            if c >= LAG:
-                second_product(c - LAG)
-        for c in range(CHUNKS - LAG, CHUNKS):
-            second_product(c)
-
+            if c == 0:
+                nc.vector.quantize_mx(out=w2_codes[:].bitcast(FP8X4), scales=w2_plane[:], in_=w2_grouped[:].rearrange("p m j -> p (m j)"))
+        inverse = sb.tile([P, S], F32, name="inverse")
         for c in range(CHUNKS):
+            second_product(c)
+        for c in range(CHUNKS):
+            if c == CHUNKS - 1:
+                for r in RATIO:
+                    nc.scalar.activation(inverse[:, r * CHUNK : (r + 1) * CHUNK], y_banks[r][:, 0:CHUNK], ACT.Exp, scale=-1.0)
             nc.scalar.activation(e0[:, PAD + c * CHUNK : PAD + (c + 1) * CHUNK], y_banks[c][:, 0:CHUNK], ACT.Exp)
 
         e2 = sb.tile([P, S], F32, name="e2")
+        ratio = sb.tile([P, S], F32, name="ratio")
         term1 = sb.tile([P, S], F32, name="term1")
         term2 = sb.tile([P, S], F32, name="term2")
 
         def sum_stage(c, stage):
             cols, lo, hi = slice(c * CHUNK, (c + 1) * CHUNK), PAD + c * CHUNK, PAD + (c + 1) * CHUNK
+            adder = nc.gpsimd if (c, stage) in GPSIMD_ADDS else nc.vector
             if stage == 0:
                 nc.vector.tensor_tensor(term1[:, cols], e0[:, lo - 1 : hi - 1], mask1[:, cols], ALU.mult)
             elif stage == 1:
-                nc.vector.tensor_tensor(e1[:, lo:hi], e0[:, lo:hi], term1[:, cols], ALU.add)
+                adder.tensor_tensor(e1[:, lo:hi], e0[:, lo:hi], term1[:, cols], ALU.add)
             elif stage == 2:
                 nc.vector.tensor_tensor(term2[:, cols], e1[:, lo - 2 : hi - 2], mask2[:, cols], ALU.mult)
-            else:
-                nc.vector.tensor_tensor(e2[:, cols], e1[:, lo:hi], term2[:, cols], ALU.add)
+            elif stage == 3:
+                adder.tensor_tensor(e2[:, cols], e1[:, lo:hi], term2[:, cols], ALU.add)
+            elif c in RATIO:
+                adder.tensor_tensor(ratio[:, cols], e2[:, cols], inverse[:, cols], ALU.mult)
 
-        ahead = [(c, stage) for stage in range(4) for c in range(CHUNKS - 1)]
+        ahead = [(c, stage) for stage in range(5) for c in range(CHUNKS - 1)]
         for i, (c, stage) in enumerate(ahead):
-            if i >= 6 and i % 2 == 0:
+            if i >= 6 and i % 2 == 0 and i <= 12:
                 sum_stage(CHUNKS - 1, (i - 6) // 2)
             sum_stage(c, stage)
-        sum_stage(CHUNKS - 1, 3)
 
         result = sb.tile([P, S], F32, name="result")
         log_sum = sb.tile([P, S], F32, name="log_sum")
-        for first, last in ((0, 2), (2, 3), (3, 4)):
-            for c in range(first, last):
+        for group in ((0, 1), (2,), (3,)):
+            for c in group:
                 cols = slice(c * CHUNK, (c + 1) * CHUNK)
-                nc.scalar.activation(log_sum[:, cols], e2[:, cols], ACT.Ln)
-                nc.vector.tensor_tensor(result[:, cols], log_sum[:, cols], y_banks[c][:, 0:CHUNK], ALU.subtract)
-            cols = slice(first * CHUNK, last * CHUNK)
+                if c in RATIO:
+                    nc.scalar.activation(result[:, cols], ratio[:, cols], ACT.Ln)
+                else:
+                    nc.scalar.activation(log_sum[:, cols], e2[:, cols], ACT.Ln)
+                    nc.vector.tensor_tensor(result[:, cols], log_sum[:, cols], y_banks[c][:, 0:CHUNK], ALU.subtract)
+            cols = slice(min(group) * CHUNK, (max(group) + 1) * CHUNK)
             nc.sync.dma_start(out[:, cols], result[:, cols])

@@ -39,7 +39,7 @@ def tile_picked_ypl_terms_p_kernel(tc, x_words, x_scales, w1, w2, in1, in2, offs
         sb = ctx.enter_context(tc.tile_pool(name="sb", bufs=1))
         psum = ctx.enter_context(tc.psum_pool(name="psum", bufs=1))
 
-        scale_table = sb.tile([P, T], U8, name="scale_table", align_bytes=64)
+        scale_table = sb.tile([P, T], U8, name="scale_table", tag="table", align_bytes=64)
         nc.sync.dma_start(scale_table[0:SCALE_ROWS, :].bitcast(I32), x_scales.rearrange("o g c -> g o c").bitcast(I32))
         nc.gpsimd.memset(scale_table[QUADRANT : 2 * QUADRANT, :].bitcast(I32), 0)
         nc.vector.memset(scale_table[2 * QUADRANT : P, :].bitcast(I32), 0)
@@ -50,7 +50,16 @@ def tile_picked_ypl_terms_p_kernel(tc, x_words, x_scales, w1, w2, in1, in2, offs
         w1_raw = [sb.tile([P, PACK, H], F32, name=f"w1_raw{o}", tag=f"stage{o}", align_bytes=64) for o in range(PASSES)]
         for o in range(PASSES):
             nc.sync.dma_start(w1_raw[o][:], w1[o * K_PASS : (o + 1) * K_PASS, :].rearrange("(p j) c -> p j c", j=PACK))
-        x_table = [sb.tile([P, T], I32, name="x_table0", align_bytes=64)]
+        picked_scales = sb.tile([P, S], U8, name="picked_scales", align_bytes=64)
+        nc.vector.tensor_copy(picked_scales[:], scale_table[:].indirect(offsets[:]))
+        rows = PASSES * PLANE_ROWS
+        for q in range(P // QUADRANT):
+            nc.sync.dma_start(
+                x_plane[QUADRANT * q : QUADRANT * q + PLANE_ROWS].rearrange("p o n -> p (o n)").bitcast(I32),
+                picked_scales[rows * q : rows * (q + 1), :].bitcast(I32),
+            )
+
+        x_table = [sb.tile([P, T], I32, name="x_table0", tag="table", align_bytes=64)]
         nc.sync.dma_start(x_table[0][:], x_words[0].rearrange("p n j -> p (n j)").bitcast(I32))
 
         e0 = sb.tile([P, PAD + S], F32, name="e0")
@@ -74,15 +83,6 @@ def tile_picked_ypl_terms_p_kernel(tc, x_words, x_scales, w1, w2, in1, in2, offs
             for c in range(CHUNKS):
                 col = i * CHUNKS + c
                 nc.tensor.transpose(mask[:, c * CHUNK : (c + 1) * CHUNK], mask_cols[:, col : col + 1].to_broadcast([P, P]), identity[:])
-
-        picked_scales = sb.tile([P, S], U8, name="picked_scales", align_bytes=64)
-        nc.vector.tensor_copy(picked_scales[:], scale_table[:].indirect(offsets[:]))
-        rows = PASSES * PLANE_ROWS
-        for q in range(P // QUADRANT):
-            nc.scalar.dma_start(
-                x_plane[QUADRANT * q : QUADRANT * q + PLANE_ROWS].rearrange("p o n -> p (o n)").bitcast(I32),
-                picked_scales[rows * q : rows * (q + 1), :].bitcast(I32),
-            )
 
         w1_codes, w1_planes = {}, {}
         for o in range(PASSES):

@@ -24,7 +24,6 @@ SCALE_ROWS = 32
 LIST_ROWS = 16
 CHUNK = 128
 CHUNKS = S // CHUNK
-HALF = 256
 PAD = 8
 BANK = 512
 VECTOR_CHUNK = 1
@@ -105,27 +104,27 @@ def tile_picked_ypl_terms_p_kernel(tc, x_words, x_scales, w1, w2, in1, in2, offs
 
         picked = {}
         for o in range(PASSES):
-            for half in range(S // HALF):
-                picked[(o, half)] = sb.tile([P, HALF], U32, name=f"picked{o}{half}", align_bytes=64)
-                entries = offsets[:, half * HALF // LIST_ROWS : (half + 1) * HALF // LIST_ROWS]
-                nc.vector.tensor_copy(picked[(o, half)][:], x_table[o][:].bitcast(U32).indirect(entries))
+            for c in range(CHUNKS):
+                picked[(o, c)] = sb.tile([P, CHUNK], U32, name=f"picked{o}{c}", align_bytes=64)
+                entries = offsets[:, c * CHUNK // LIST_ROWS : (c + 1) * CHUNK // LIST_ROWS]
+                nc.vector.tensor_copy(picked[(o, c)][:], x_table[o][:].bitcast(U32).indirect(entries))
 
-        w2_grouped = sb.tile([P, N, PACK], BF16, name="w2_grouped", tag="stage0", align_bytes=64)
-        nc.gpsimd.tensor_scalar(w2_grouped[:], w2_raw[:].rearrange("p j m -> p m j"), 1.0, 0.0, ALU.mult, ALU.add)
+        w2_grouped = sb.tile([P, N, PACK], BF16, name="w2_grouped", align_bytes=64)
+        nc.scalar.copy(w2_grouped[:], w2_raw[:].rearrange("p j m -> p m j"))
         w2_codes = sb.tile([P, N], U32, name="w2_codes", align_bytes=64)
         w2_plane = sb.tile([P, N], U8, name="w2_plane", align_bytes=64)
+        nc.vector.quantize_mx(out=w2_codes[:].bitcast(FP8X4), scales=w2_plane[:], in_=w2_grouped[:].rearrange("p m j -> p (m j)"))
 
         h_banks = [psum.tile([P, PACK, CHUNK], F32, name=f"h_bank{c}", tag=f"bank{c}") for c in range(CHUNKS)]
         y_banks = {}
         h_quantised = []
 
         def first_product(c, t, o):
-            half, first = divmod(c * CHUNK, HALF)
             nc.tensor.matmul_mx(
                 out=h_banks[c][:, t, :],
                 lhsT=w1_codes[(o, t)].bitcast(FP8X4),
                 lhsT_scale=w1_planes[(o, t)],
-                rhs=picked[(o, half)][:, first : first + CHUNK].bitcast(FP8X4),
+                rhs=picked[(o, c)][:].bitcast(FP8X4),
                 rhs_scale=x_plane[:, o, c * CHUNK : (c + 1) * CHUNK],
                 start=(o == 0 and t == 0),
                 stop=(o == PASSES - 1 and t == PACK - 1),
@@ -161,8 +160,6 @@ def tile_picked_ypl_terms_p_kernel(tc, x_words, x_scales, w1, w2, in1, in2, offs
             h_plane = sb.tile([P, CHUNK], U8, name=f"h_plane{c}", align_bytes=64)
             nc.vector.quantize_mx(out=h_codes[:].bitcast(FP8X4), scales=h_plane[:], in_=h_grouped[c][:].rearrange("p n t -> p (n t)"))
             h_quantised.append((h_codes, h_plane))
-            if c == 0:
-                nc.vector.quantize_mx(out=w2_codes[:].bitcast(FP8X4), scales=w2_plane[:], in_=w2_grouped[:].rearrange("p m j -> p (m j)"))
         inverse = sb.tile([P, S], F32, name="inverse")
         for c in range(CHUNKS):
             second_product(c)

@@ -110,7 +110,7 @@ def tile_picked_ypl_terms_p_kernel(tc, x_words, x_scales, w1, w2, in1, in2, offs
                 nc.vector.tensor_copy(picked[(o, c)][:], x_table[o][:].bitcast(U32).indirect(entries))
 
         w2_grouped = sb.tile([P, N, PACK], BF16, name="w2_grouped", align_bytes=64)
-        nc.scalar.copy(w2_grouped[:], w2_raw[:].rearrange("p j m -> p m j"))
+        nc.scalar.copy(w2_grouped[:].rearrange("p (c i) j -> p c j i", i=4), w2_raw[:].rearrange("p j (c i) -> p c j i", i=4))
         w2_codes = sb.tile([P, N], U32, name="w2_codes", align_bytes=64)
         w2_plane = sb.tile([P, N], U8, name="w2_plane", align_bytes=64)
         nc.vector.quantize_mx(out=w2_codes[:].bitcast(FP8X4), scales=w2_plane[:], in_=w2_grouped[:].rearrange("p m j -> p (m j)"))

@@ -26,9 +26,12 @@ CHUNK = 128
 CHUNKS = S // CHUNK
 PAD = 8
 BANK = 512
+LINE = 4
+SUM_STAGES = 4
 VECTOR_CHUNK = 1
-GPSIMD_ADDS = ()
-RATIO = ()
+VECTOR_COLUMNS = 80
+HEAD_STAGES = 2
+STORES = ((0, 1), (2,), (3,))
 FLOPS = 2 * K * H * S + 2 * H * N * S
 
 
@@ -70,36 +73,37 @@ def tile_picked_ypl_terms_p_kernel(tc, x_words, x_scales, w1, w2, in1, in2, offs
         nc.gpsimd.memset(mask_rows[:], 0.0)
         identity = sb.tile([P, P], F32, name="identity")
         make_identity(nc, identity[:])
-        for i, mask in enumerate((in1, in2)):
-            nc.scalar.dma_start(mask_rows[i * CHUNKS : (i + 1) * CHUNKS, :], mask[0].rearrange("(c n) -> c n", c=CHUNKS))
+        for i, mask_input in enumerate((in1, in2)):
+            nc.scalar.dma_start(mask_rows[i * CHUNKS : (i + 1) * CHUNKS, :], mask_input[0].rearrange("(c n) -> c n", c=CHUNKS))
         turned = psum.tile([P, BANK], F32, name="turned", tag="bank0")
         nc.tensor.transpose(turned[:, 0:P], mask_rows[:], identity[:])
-        mask_cols = sb.tile([P, 2 * CHUNKS], F32, name="mask_cols")
-        nc.scalar.copy(mask_cols[:], turned[:, 0 : 2 * CHUNKS])
-        mask1 = psum.tile([P, S], F32, name="mask1")
-        mask2 = psum.tile([P, S], F32, name="mask2")
-        for i, mask in enumerate((mask1, mask2)):
-            for c in range(CHUNKS):
-                col = i * CHUNKS + c
-                nc.tensor.transpose(mask[:, c * CHUNK : (c + 1) * CHUNK], mask_cols[:, col : col + 1].to_broadcast([P, P]), identity[:])
 
         w1_codes, w1_planes = {}, {}
         for o in range(PASSES):
-            dealt = w1_raw[o][:].rearrange("p j (m u v) -> p u m v j", u=2, v=2)
-            for u in range(2):
-                grouped = sb.tile([P, 2, P, PACK], BF16, name=f"w1_grouped{o}{u}", align_bytes=64)
-                interleave = nc.vector.tensor_copy if u == 0 else nc.scalar.copy
-                interleave(grouped[:].rearrange("p v m j -> p m v j"), dealt[:, u])
-                codes = sb.tile([P, 2 * P], U32, name=f"w1_codes{o}{u}", align_bytes=64)
-                plane = sb.tile([P, 2 * P], U8, name=f"w1_plane{o}{u}", align_bytes=64)
-                nc.vector.quantize_mx(out=codes[:].bitcast(FP8X4), scales=plane[:], in_=grouped[:].rearrange("p v m j -> p (v m j)"))
-                for v in range(2):
-                    w1_codes[(o, 2 * u + v)] = codes[:, v * P : (v + 1) * P]
-                    w1_planes[(o, 2 * u + v)] = plane[:, v * P : (v + 1) * P]
+            dealt = w1_raw[o][:].rearrange("p j (m t) -> p m j t", t=PACK)
+            grouped = sb.tile([P, PACK, P, PACK], BF16, name=f"w1_grouped{o}", tag=f"grouped{o}", align_bytes=64)
+            target = grouped[:].rearrange("p t m j -> p m j t")
+            nc.vector.tensor_copy(target[:, 0:VECTOR_COLUMNS], dealt[:, 0:VECTOR_COLUMNS])
+            nc.scalar.copy(target[:, VECTOR_COLUMNS:P], dealt[:, VECTOR_COLUMNS:P])
+            codes = sb.tile([P, PACK * P], U32, name=f"w1_codes{o}", align_bytes=64)
+            plane = sb.tile([P, PACK * P], U8, name=f"w1_plane{o}", align_bytes=64)
+            nc.vector.quantize_mx(out=codes[:].bitcast(FP8X4), scales=plane[:], in_=grouped[:].rearrange("p t m j -> p (t m j)"))
+            for t in range(PACK):
+                w1_codes[(o, t)] = codes[:, t * P : (t + 1) * P]
+                w1_planes[(o, t)] = plane[:, t * P : (t + 1) * P]
+
+        mask_cols = sb.tile([P, 2 * CHUNKS], F32, name="mask_cols", tag="stage1", align_bytes=64)
+        nc.scalar.copy(mask_cols[:], turned[:, 0 : 2 * CHUNKS])
+        mask1 = psum.tile([P, S], F32, name="mask1")
+        mask2 = psum.tile([P, S], F32, name="mask2")
+        for i, spread in enumerate((mask1, mask2)):
+            for c in range(CHUNKS):
+                col = i * CHUNKS + c
+                nc.tensor.transpose(spread[:, c * CHUNK : (c + 1) * CHUNK], mask_cols[:, col : col + 1].to_broadcast([P, P]), identity[:])
 
         x_table.append(sb.tile([P, T], I32, name="x_table1", tag="stage0", align_bytes=64))
         nc.sync.dma_start(x_table[1][:], x_words[1].rearrange("p n j -> p (n j)").bitcast(I32))
-        w2_raw = sb.tile([P, PACK, N], F32, name="w2_raw", tag="stage1", align_bytes=64)
+        w2_raw = sb.tile([P, PACK, N], F32, name="w2_raw", tag="grouped1", align_bytes=64)
         nc.sync.dma_start(w2_raw[:], w2.rearrange("(p j) m -> p j m", j=PACK))
 
         picked = {}
@@ -110,29 +114,42 @@ def tile_picked_ypl_terms_p_kernel(tc, x_words, x_scales, w1, w2, in1, in2, offs
                 nc.vector.tensor_copy(picked[(o, c)][:], x_table[o][:].bitcast(U32).indirect(entries))
 
         w2_grouped = sb.tile([P, N, PACK], BF16, name="w2_grouped", align_bytes=64)
-        nc.scalar.copy(w2_grouped[:].rearrange("p (c i) j -> p c j i", i=4), w2_raw[:].rearrange("p j (c i) -> p c j i", i=4))
+        nc.scalar.copy(w2_grouped[:].rearrange("p (c i) j -> p c j i", i=LINE), w2_raw[:].rearrange("p j (c i) -> p c j i", i=LINE))
         w2_codes = sb.tile([P, N], U32, name="w2_codes", align_bytes=64)
         w2_plane = sb.tile([P, N], U8, name="w2_plane", align_bytes=64)
         nc.vector.quantize_mx(out=w2_codes[:].bitcast(FP8X4), scales=w2_plane[:], in_=w2_grouped[:].rearrange("p m j -> p (m j)"))
 
         h_banks = [psum.tile([P, PACK, CHUNK], F32, name=f"h_bank{c}", tag=f"bank{c}") for c in range(CHUNKS)]
-        y_banks = {}
+        for o in range(PASSES):
+            for c in range(CHUNKS):
+                for t in range(PACK):
+                    nc.tensor.matmul_mx(
+                        out=h_banks[c][:, t, :],
+                        lhsT=w1_codes[(o, t)].bitcast(FP8X4),
+                        lhsT_scale=w1_planes[(o, t)],
+                        rhs=picked[(o, c)][:].bitcast(FP8X4),
+                        rhs_scale=x_plane[:, o, c * CHUNK : (c + 1) * CHUNK],
+                        start=(o == 0 and t == 0),
+                        stop=(o == PASSES - 1 and t == PACK - 1),
+                    )
+
+        h_grouped = []
+        for c in range(CHUNKS):
+            h_grouped.append(sb.tile([P, CHUNK, PACK], BF16, name=f"h_grouped{c}", align_bytes=64))
+            if c == VECTOR_CHUNK:
+                nc.vector.tensor_scalar_max(h_grouped[c][:], h_banks[c][:].rearrange("p t n -> p n t"), 0.0)
+            else:
+                nc.scalar.activation(h_grouped[c][:], h_banks[c][:].rearrange("p t n -> p n t"), ACT.Relu)
         h_quantised = []
+        for c in range(CHUNKS):
+            h_codes = sb.tile([P, CHUNK], U32, name=f"h_codes{c}", align_bytes=64)
+            h_plane = sb.tile([P, CHUNK], U8, name=f"h_plane{c}", align_bytes=64)
+            nc.vector.quantize_mx(out=h_codes[:].bitcast(FP8X4), scales=h_plane[:], in_=h_grouped[c][:].rearrange("p n t -> p (n t)"))
+            h_quantised.append((h_codes, h_plane))
 
-        def first_product(c, t, o):
-            nc.tensor.matmul_mx(
-                out=h_banks[c][:, t, :],
-                lhsT=w1_codes[(o, t)].bitcast(FP8X4),
-                lhsT_scale=w1_planes[(o, t)],
-                rhs=picked[(o, c)][:].bitcast(FP8X4),
-                rhs_scale=x_plane[:, o, c * CHUNK : (c + 1) * CHUNK],
-                start=(o == 0 and t == 0),
-                stop=(o == PASSES - 1 and t == PACK - 1),
-            )
-
-        def second_product(c):
-            h_codes, h_plane = h_quantised[c]
-            y_banks[c] = psum.tile([P, BANK], F32, name=f"y_bank{c}", tag=f"bank{c}")
+        y_banks = []
+        for c, (h_codes, h_plane) in enumerate(h_quantised):
+            y_banks.append(psum.tile([P, BANK], F32, name=f"y_bank{c}", tag=f"bank{c}"))
             nc.tensor.matmul_mx(
                 out=y_banks[c][:, 0:CHUNK],
                 lhsT=w2_codes[:].bitcast(FP8X4),
@@ -142,67 +159,39 @@ def tile_picked_ypl_terms_p_kernel(tc, x_words, x_scales, w1, w2, in1, in2, offs
                 start=True,
                 stop=True,
             )
-
-        for o in range(PASSES):
-            for c in range(CHUNKS):
-                for t in range(PACK):
-                    first_product(c, t, o)
-
-        h_grouped = []
         for c in range(CHUNKS):
-            h_grouped.append(sb.tile([P, CHUNK, PACK], BF16, name=f"h_grouped{c}", align_bytes=64))
-            if c == VECTOR_CHUNK:
-                nc.vector.tensor_scalar_max(h_grouped[c][:], h_banks[c][:].rearrange("p t n -> p n t"), 0.0)
-            else:
-                nc.scalar.activation(h_grouped[c][:], h_banks[c][:].rearrange("p t n -> p n t"), ACT.Relu)
-        for c in range(CHUNKS):
-            h_codes = sb.tile([P, CHUNK], U32, name=f"h_codes{c}", align_bytes=64)
-            h_plane = sb.tile([P, CHUNK], U8, name=f"h_plane{c}", align_bytes=64)
-            nc.vector.quantize_mx(out=h_codes[:].bitcast(FP8X4), scales=h_plane[:], in_=h_grouped[c][:].rearrange("p n t -> p (n t)"))
-            h_quantised.append((h_codes, h_plane))
-        inverse = sb.tile([P, S], F32, name="inverse")
-        for c in range(CHUNKS):
-            second_product(c)
-        for c in range(CHUNKS):
-            if c == CHUNKS - 1:
-                for r in RATIO:
-                    nc.scalar.activation(inverse[:, r * CHUNK : (r + 1) * CHUNK], y_banks[r][:, 0:CHUNK], ACT.Exp, scale=-1.0)
             nc.scalar.activation(e0[:, PAD + c * CHUNK : PAD + (c + 1) * CHUNK], y_banks[c][:, 0:CHUNK], ACT.Exp)
 
         e2 = sb.tile([P, S], F32, name="e2")
-        ratio = sb.tile([P, S], F32, name="ratio")
         term1 = sb.tile([P, S], F32, name="term1")
         term2 = sb.tile([P, S], F32, name="term2")
 
         def sum_stage(c, stage):
             cols, lo, hi = slice(c * CHUNK, (c + 1) * CHUNK), PAD + c * CHUNK, PAD + (c + 1) * CHUNK
-            adder = nc.gpsimd if (c, stage) in GPSIMD_ADDS else nc.vector
             if stage == 0:
                 nc.vector.tensor_tensor(term1[:, cols], e0[:, lo - 1 : hi - 1], mask1[:, cols], ALU.mult)
             elif stage == 1:
-                adder.tensor_tensor(e1[:, lo:hi], e0[:, lo:hi], term1[:, cols], ALU.add)
+                nc.vector.tensor_tensor(e1[:, lo:hi], e0[:, lo:hi], term1[:, cols], ALU.add)
             elif stage == 2:
                 nc.vector.tensor_tensor(term2[:, cols], e1[:, lo - 2 : hi - 2], mask2[:, cols], ALU.mult)
-            elif stage == 3:
-                adder.tensor_tensor(e2[:, cols], e1[:, lo:hi], term2[:, cols], ALU.add)
-            elif c in RATIO:
-                adder.tensor_tensor(ratio[:, cols], e2[:, cols], inverse[:, cols], ALU.mult)
+            else:
+                nc.vector.tensor_tensor(e2[:, cols], e1[:, lo:hi], term2[:, cols], ALU.add)
 
-        ahead = [(c, stage) for stage in range(5) for c in range(CHUNKS - 1)]
-        for i, (c, stage) in enumerate(ahead):
-            if i >= 6 and i % 2 == 0 and i <= 12:
-                sum_stage(CHUNKS - 1, (i - 6) // 2)
-            sum_stage(c, stage)
+        for stage in range(HEAD_STAGES):
+            for c in range(CHUNKS - 1):
+                sum_stage(c, stage)
+        left = [(c, stage) for stage in range(HEAD_STAGES, SUM_STAGES) for c in range(CHUNKS - 1)]
+        for stage in range(SUM_STAGES):
+            sum_stage(CHUNKS - 1, stage)
+            for c, other_stage in left[2 * stage : 2 * stage + 2]:
+                sum_stage(c, other_stage)
 
         result = sb.tile([P, S], F32, name="result")
         log_sum = sb.tile([P, S], F32, name="log_sum")
-        for group in ((0, 1), (2,), (3,)):
+        for group in STORES:
             for c in group:
                 cols = slice(c * CHUNK, (c + 1) * CHUNK)
-                if c in RATIO:
-                    nc.scalar.activation(result[:, cols], ratio[:, cols], ACT.Ln)
-                else:
-                    nc.scalar.activation(log_sum[:, cols], e2[:, cols], ACT.Ln)
-                    nc.vector.tensor_tensor(result[:, cols], log_sum[:, cols], y_banks[c][:, 0:CHUNK], ALU.subtract)
-            cols = slice(min(group) * CHUNK, (max(group) + 1) * CHUNK)
-            nc.sync.dma_start(out[:, cols], result[:, cols])
+                nc.scalar.activation(log_sum[:, cols], e2[:, cols], ACT.Ln)
+                nc.vector.tensor_tensor(result[:, cols], log_sum[:, cols], y_banks[c][:, 0:CHUNK], ALU.subtract)
+            stored = slice(min(group) * CHUNK, (max(group) + 1) * CHUNK)
+            nc.sync.dma_start(out[:, stored], result[:, stored])

from contextlib import ExitStack

import concourse.mybir as mybir
from concourse.masks import make_identity

F32 = mybir.dt.float32
BF16 = mybir.dt.bfloat16
I32 = mybir.dt.int32
U32 = mybir.dt.uint32
U16 = mybir.dt.uint16
U8 = mybir.dt.uint8
FP8X4 = mybir.dt.float8_e4m3fn_x4
ACT = mybir.ActivationFunctionType
ALU = mybir.AluOpType

K, T, S, H, N = 1024, 2048, 512, 512, 128
P = 128
PACK = 4
K_PASS = P * PACK
PASSES = K // K_PASS
QUADRANT = 32
PLANE_ROWS = 4
SCALE_ROWS = 32
LIST_ROWS = 16
CHUNK = 128
CHUNKS = S // CHUNK
PAD = 8
BANK = 512
LINE = 4
SUM_STAGES = 4
VECTOR_CHUNK = 1
VECTOR_COLUMNS = 80
HEAD_STAGES = 2
STORES = ((0, 1), (2,), (3,))
FLOPS = 2 * K * H * S + 2 * H * N * S


def tile_picked_ypl_terms_p_kernel(tc, x_words, x_scales, w1, w2, in1, in2, offs, out):
    nc = tc.nc
    with ExitStack() as ctx:
        sb = ctx.enter_context(tc.tile_pool(name="sb", bufs=1))
        psum = ctx.enter_context(tc.psum_pool(name="psum", bufs=1))

        scale_table = sb.tile([P, T], U8, name="scale_table", tag="table", align_bytes=64)
        nc.sync.dma_start(scale_table[0:SCALE_ROWS, :].bitcast(I32), x_scales.rearrange("o g c -> g o c").bitcast(I32))
        nc.gpsimd.memset(scale_table[QUADRANT : 2 * QUADRANT, :].bitcast(I32), 0)
        nc.vector.memset(scale_table[2 * QUADRANT : P, :].bitcast(I32), 0)
        x_plane = sb.tile([P, PASSES, S], U8, name="x_plane", align_bytes=64)
        nc.gpsimd.memset(x_plane[:].rearrange("p o n -> p (o n)").bitcast(I32), 0)
        offsets = sb.tile([P, S // LIST_ROWS], U16, name="offsets")
        nc.sync.dma_start(offsets[:], offs)
        w1_raw = [sb.tile([P, PACK, H], F32, name=f"w1_raw{o}", tag=f"stage{o}", align_bytes=64) for o in range(PASSES)]
        for o in range(PASSES):
            nc.sync.dma_start(w1_raw[o][:], w1[o * K_PASS : (o + 1) * K_PASS, :].rearrange("(p j) c -> p j c", j=PACK))
        picked_scales = sb.tile([P, S], U8, name="picked_scales", align_bytes=64)
        nc.vector.tensor_copy(picked_scales[:], scale_table[:].indirect(offsets[:]))
        rows = PASSES * PLANE_ROWS
        for q in range(P // QUADRANT):
            nc.sync.dma_start(
                x_plane[QUADRANT * q : QUADRANT * q + PLANE_ROWS].rearrange("p o n -> p (o n)").bitcast(I32),
                picked_scales[rows * q : rows * (q + 1), :].bitcast(I32),
            )

        x_table = [sb.tile([P, T], I32, name="x_table0", tag="table", align_bytes=64)]
        nc.sync.dma_start(x_table[0][:], x_words[0].rearrange("p n j -> p (n j)").bitcast(I32))

        e0 = sb.tile([P, PAD + S], F32, name="e0")
        e1 = sb.tile([P, PAD + S], F32, name="e1")
        nc.vector.memset(e1[:, 0:PAD], 0.0)
        nc.scalar.copy(e0[:, 0:PAD], e1[:, 0:PAD])

        mask_rows = sb.tile([P, CHUNK], F32, name="mask_rows")
        nc.gpsimd.memset(mask_rows[:], 0.0)
        identity = sb.tile([P, P], F32, name="identity")
        make_identity(nc, identity[:])
        for i, mask_input in enumerate((in1, in2)):
            nc.scalar.dma_start(mask_rows[i * CHUNKS : (i + 1) * CHUNKS, :], mask_input[0].rearrange("(c n) -> c n", c=CHUNKS))
        turned = psum.tile([P, BANK], F32, name="turned", tag="bank0")
        nc.tensor.transpose(turned[:, 0:P], mask_rows[:], identity[:])

        w1_codes, w1_planes = {}, {}
        for o in range(PASSES):
            dealt = w1_raw[o][:].rearrange("p j (m t) -> p m j t", t=PACK)
            grouped = sb.tile([P, PACK, P, PACK], BF16, name=f"w1_grouped{o}", tag=f"grouped{o}", align_bytes=64)
            target = grouped[:].rearrange("p t m j -> p m j t")
            nc.vector.tensor_copy(target[:, 0:VECTOR_COLUMNS], dealt[:, 0:VECTOR_COLUMNS])
            nc.scalar.copy(target[:, VECTOR_COLUMNS:P], dealt[:, VECTOR_COLUMNS:P])
            codes = sb.tile([P, PACK * P], U32, name=f"w1_codes{o}", align_bytes=64)
            plane = sb.tile([P, PACK * P], U8, name=f"w1_plane{o}", align_bytes=64)
            nc.vector.quantize_mx(out=codes[:].bitcast(FP8X4), scales=plane[:], in_=grouped[:].rearrange("p t m j -> p (t m j)"))
            for t in range(PACK):
                w1_codes[(o, t)] = codes[:, t * P : (t + 1) * P]
                w1_planes[(o, t)] = plane[:, t * P : (t + 1) * P]

        mask_cols = sb.tile([P, 2 * CHUNKS], F32, name="mask_cols", tag="stage1", align_bytes=64)
        nc.scalar.copy(mask_cols[:], turned[:, 0 : 2 * CHUNKS])
        mask1 = psum.tile([P, S], F32, name="mask1")
        mask2 = psum.tile([P, S], F32, name="mask2")
        for i, spread in enumerate((mask1, mask2)):
            for c in range(CHUNKS):
                col = i * CHUNKS + c
                nc.tensor.transpose(spread[:, c * CHUNK : (c + 1) * CHUNK], mask_cols[:, col : col + 1].to_broadcast([P, P]), identity[:])

        x_table.append(sb.tile([P, T], I32, name="x_table1", tag="stage0", align_bytes=64))
        nc.sync.dma_start(x_table[1][:], x_words[1].rearrange("p n j -> p (n j)").bitcast(I32))
        w2_raw = sb.tile([P, PACK, N], F32, name="w2_raw", tag="grouped1", align_bytes=64)
        nc.sync.dma_start(w2_raw[:], w2.rearrange("(p j) m -> p j m", j=PACK))

        picked = {}
        for o in range(PASSES):
            for c in range(CHUNKS):
                picked[(o, c)] = sb.tile([P, CHUNK], U32, name=f"picked{o}{c}", align_bytes=64)
                entries = offsets[:, c * CHUNK // LIST_ROWS : (c + 1) * CHUNK // LIST_ROWS]
                nc.vector.tensor_copy(picked[(o, c)][:], x_table[o][:].bitcast(U32).indirect(entries))

        w2_grouped = sb.tile([P, N, PACK], BF16, name="w2_grouped", align_bytes=64)
        nc.scalar.copy(w2_grouped[:].rearrange("p (c i) j -> p c j i", i=LINE), w2_raw[:].rearrange("p j (c i) -> p c j i", i=LINE))
        w2_codes = sb.tile([P, N], U32, name="w2_codes", align_bytes=64)
        w2_plane = sb.tile([P, N], U8, name="w2_plane", align_bytes=64)
        nc.vector.quantize_mx(out=w2_codes[:].bitcast(FP8X4), scales=w2_plane[:], in_=w2_grouped[:].rearrange("p m j -> p (m j)"))

        h_banks = [psum.tile([P, PACK, CHUNK], F32, name=f"h_bank{c}", tag=f"bank{c}") for c in range(CHUNKS)]
        for o in range(PASSES):
            for c in range(CHUNKS):
                for t in range(PACK):
                    nc.tensor.matmul_mx(
                        out=h_banks[c][:, t, :],
                        lhsT=w1_codes[(o, t)].bitcast(FP8X4),
                        lhsT_scale=w1_planes[(o, t)],
                        rhs=picked[(o, c)][:].bitcast(FP8X4),
                        rhs_scale=x_plane[:, o, c * CHUNK : (c + 1) * CHUNK],
                        start=(o == 0 and t == 0),
                        stop=(o == PASSES - 1 and t == PACK - 1),
                    )

        h_grouped = []
        for c in range(CHUNKS):
            h_grouped.append(sb.tile([P, CHUNK, PACK], BF16, name=f"h_grouped{c}", align_bytes=64))
            if c == VECTOR_CHUNK:
                nc.vector.tensor_scalar_max(h_grouped[c][:], h_banks[c][:].rearrange("p t n -> p n t"), 0.0)
            else:
                nc.scalar.activation(h_grouped[c][:], h_banks[c][:].rearrange("p t n -> p n t"), ACT.Relu)
        h_quantised = []
        for c in range(CHUNKS):
            h_codes = sb.tile([P, CHUNK], U32, name=f"h_codes{c}", align_bytes=64)
            h_plane = sb.tile([P, CHUNK], U8, name=f"h_plane{c}", align_bytes=64)
            nc.vector.quantize_mx(out=h_codes[:].bitcast(FP8X4), scales=h_plane[:], in_=h_grouped[c][:].rearrange("p n t -> p (n t)"))
            h_quantised.append((h_codes, h_plane))

        y_banks = []
        for c, (h_codes, h_plane) in enumerate(h_quantised):
            y_banks.append(psum.tile([P, BANK], F32, name=f"y_bank{c}", tag=f"bank{c}"))
            nc.tensor.matmul_mx(
                out=y_banks[c][:, 0:CHUNK],
                lhsT=w2_codes[:].bitcast(FP8X4),
                lhsT_scale=w2_plane[:],
                rhs=h_codes[:].bitcast(FP8X4),
                rhs_scale=h_plane[:],
                start=True,
                stop=True,
            )
        for c in range(CHUNKS):
            nc.scalar.activation(e0[:, PAD + c * CHUNK : PAD + (c + 1) * CHUNK], y_banks[c][:, 0:CHUNK], ACT.Exp)

        e2 = sb.tile([P, S], F32, name="e2")
        term1 = sb.tile([P, S], F32, name="term1")
        term2 = sb.tile([P, S], F32, name="term2")

        def sum_stage(c, stage):
            cols, lo, hi = slice(c * CHUNK, (c + 1) * CHUNK), PAD + c * CHUNK, PAD + (c + 1) * CHUNK
            if stage == 0:
                nc.vector.tensor_tensor(term1[:, cols], e0[:, lo - 1 : hi - 1], mask1[:, cols], ALU.mult)
            elif stage == 1:
                nc.vector.tensor_tensor(e1[:, lo:hi], e0[:, lo:hi], term1[:, cols], ALU.add)
            elif stage == 2:
                nc.vector.tensor_tensor(term2[:, cols], e1[:, lo - 2 : hi - 2], mask2[:, cols], ALU.mult)
            else:
                nc.vector.tensor_tensor(e2[:, cols], e1[:, lo:hi], term2[:, cols], ALU.add)

        for stage in range(HEAD_STAGES):
            for c in range(CHUNKS - 1):
                sum_stage(c, stage)
        left = [(c, stage) for stage in range(HEAD_STAGES, SUM_STAGES) for c in range(CHUNKS - 1)]
        for stage in range(SUM_STAGES):
            sum_stage(CHUNKS - 1, stage)
            for c, other_stage in left[2 * stage : 2 * stage + 2]:
                sum_stage(c, other_stage)

        result = sb.tile([P, S], F32, name="result")
        log_sum = sb.tile([P, S], F32, name="log_sum")
        for group in STORES:
            for c in group:
                cols = slice(c * CHUNK, (c + 1) * CHUNK)
                nc.scalar.activation(log_sum[:, cols], e2[:, cols], ACT.Ln)
                nc.vector.tensor_tensor(result[:, cols], log_sum[:, cols], y_banks[c][:, 0:CHUNK], ALU.subtract)
            stored = slice(min(group) * CHUNK, (max(group) + 1) * CHUNK)
            nc.sync.dma_start(out[:, stored], result[:, stored])
